import numpy as np
import ml_dtypes


def mxq(x, axis, fmt="e4m3"):
    dtype, down = {"e4m3": (ml_dtypes.float8_e4m3fn, 7), "e5m2": (ml_dtypes.float8_e5m2, 14)}[fmt]
    v = np.moveaxis(np.asarray(x, np.float32).astype(ml_dtypes.bfloat16).astype(np.float64), axis, -1)
    blocks = v.reshape(v.shape[:-1] + (-1, 32))
    amax = np.abs(blocks).max(-1, keepdims=True)
    byte = np.maximum(np.where(amax > 0, np.frexp(amax)[1] - 1 + 127, 0) - down, 1)
    scale = np.exp2(byte - 127.0)
    codes = (blocks / scale).astype(np.float32).astype(dtype).astype(np.float64)
    return np.moveaxis((codes * scale).reshape(v.shape), -1, axis)


WIDE = False


def mx_kscale(k):
    if not WIDE:
        return np.ones(k)
    levels = np.array([10, -10, 5, -5, 0])
    if k % 512:
        return np.exp2(np.random.permutation(np.resize(levels, k // 32))).repeat(32)
    a = np.empty((k // 512, 16))
    for p in range(k // 512):
        a[p, :8] = np.random.permutation(np.resize(levels, 8))
        for g in range(8):
            far = levels[np.abs(levels - a[p, g]) >= 10]
            a[p, g + 8] = far[np.random.randint(len(far))]
    return np.exp2(a.ravel()).repeat(32)


def f64(x):
    return np.asarray(x).astype(np.float64)


def striped(idx):
    return np.tile(np.asarray(idx).reshape(-1, 16).T, (8, 1)).astype(np.uint16)


def unstriped(offs):
    return offs[:16].T.reshape(-1).astype(np.int64)


E2M1 = np.array([0.0, 0.5, 1.0, 1.5, 2.0, 3.0, 4.0, 6.0, -0.0, -0.5, -1.0, -1.5, -2.0, -3.0, -4.0, -6.0])


def pack_weight(w, fmt):
    k, n = w.shape
    w = f64(np.asarray(w, np.float32).astype(ml_dtypes.bfloat16)).reshape(k // 32, 32, n)
    amax = np.abs(w).max(1)
    if fmt == "e4m3":
        byte = np.frexp(amax)[1] - 1 + 127 - 7
    else:
        mant, ex = np.frexp(amax / 6.0)
        byte = np.where(mant > 0.5, ex, ex - 1) + 127
    byte = np.clip(np.where(amax > 0, byte, 1), 1, 254)
    scaled = (w * np.exp2(127.0 - byte)[:, None, :]).reshape(k, n).astype(np.float32)
    by_word = np.ascontiguousarray(scaled.reshape(k // 512, 128, 4, n).transpose(0, 1, 3, 2))
    if fmt == "e4m3":
        words = by_word.astype(ml_dtypes.float8_e4m3fn).view(np.uint8)
    else:
        c = by_word.astype(ml_dtypes.float4_e2m1fn).view(np.uint8) & 0xF
        words = (c[..., 0::2] | (c[..., 1::2] << 4)).reshape(k // 512, 128, 2 * n)
    return np.ascontiguousarray(words), np.ascontiguousarray(byte.astype(np.uint8).reshape(k // 512, 16, n))


def unpack_weight(words, scales, fmt):
    g, _, n = scales.shape
    words = np.ascontiguousarray(words).reshape(g, 128, n, -1)
    if fmt == "e4m3":
        vals = words.view(ml_dtypes.float8_e4m3fn).astype(np.float64)
    else:
        nib = np.empty((g, 128, n, 4), np.uint8)
        nib[..., 0::2] = words & 0xF
        nib[..., 1::2] = words >> 4
        vals = E2M1[nib]
    vals = vals * np.repeat(np.exp2(scales.astype(np.float64) - 127.0), 8, axis=1)[..., None]
    return vals.transpose(0, 1, 3, 2).reshape(g * 512, n)


def bf(x):
    return np.asarray(x, np.float32).astype(ml_dtypes.bfloat16)


def planes(Y):
    r, m = Y.shape
    b = f64(bf(Y)).reshape(r // 32, 32, m)
    amax = np.abs(b).max(1)
    byte = np.clip(np.where(amax > 0, np.frexp(amax)[1] - 1 + 127 - 7, 1), 1, 254)
    codes = (b * np.exp2(127.0 - byte)[:, None, :]).reshape(r, m).astype(np.float32).astype(ml_dtypes.float8_e4m3fn).view(np.uint8)
    words = codes.reshape(r // 512, 128, 4, m).transpose(0, 1, 3, 2)
    return np.ascontiguousarray(words), np.ascontiguousarray(byte.astype(np.uint8).reshape(r // 512, 16, m))


D, T, I, Q, E, M = 512, 2048, 512, 256, 512, 1024


def setup_inputs():
    n = np.random.standard_normal
    idx = np.random.permutation(T)[:I]
    idx2 = np.random.permutation(T)[:I]
    idx3 = np.random.permutation(T)[:I]
    idx4 = np.random.permutation(M)[:Q]
    fd = mx_kscale(D)
    fi = mx_kscale(I)
    ti = np.ones(T)
    ti[idx] = fi
    keysp = pack_weight(n((D, T)) / fd[:, None], "e2m1")
    return {
        "query": (n((D, Q)) * 1.2 / np.sqrt(D) * fd[:, None]).astype(np.float32),
        "keys_words": keysp[0],
        "keys_scales": keysp[1],
        "lam": (np.random.uniform(0.8, 1.8, (Q, 1))).astype(np.float32),
        "os": (np.random.uniform(0.02, 0.08, (1, I)) * fi).astype(np.float32),
        "vals": (n((E, T)) / ti).astype(np.float32),
        "member": (n((E, M))).astype(np.float32),
        "mgain": np.tile(np.random.uniform(0.5, 2.0, M), (128, 1)).astype(np.float32),
        "offs": striped(idx),
        "offs2": striped(idx2),
        "offs3": striped(idx3),
        "offs4": striped(idx4),
    }


def reference(query, keys_words, keys_scales, lam, os, vals, member, mgain, offs, offs2, offs3, offs4):
    idx = unstriped(offs)
    idx2 = unstriped(offs2)
    idx3 = unstriped(offs3)
    idx4 = unstriped(offs4)
    keysu = unpack_weight(keys_words, keys_scales, "e2m1")
    queryq = mxq(f64(query), 0, "e4m3")
    a = queryq.T @ keysu
    lo2 = np.minimum(a[:, idx], a[:, idx2])
    hi2 = np.maximum(a[:, idx], a[:, idx2])
    s = np.maximum(lo2, np.minimum(hi2, a[:, idx3])) * f64(lam)
    w = np.maximum(s, 0.0)
    wo1 = w * f64(os)
    wt1 = wo1.T
    vt1 = f64(vals)[:, idx].T
    vt1q = mxq(vt1, 0, "e4m3")
    wt1q = mxq(wt1, 0, "e4m3")
    o = vt1q.T @ wt1q
    y = o * f64(mgain)[:1][:, idx4] + f64(member)[:, idx4]
    words, scales = planes(y)
    return y, words, scales

@@ -1,0 +1,239 @@
+from contextlib import ExitStack
+
+import concourse.mybir as mybir
+from concourse.masks import make_identity
+
+F32 = mybir.dt.float32
+BF16 = mybir.dt.bfloat16
+I32 = mybir.dt.int32
+U32 = mybir.dt.uint32
+U16 = mybir.dt.uint16
+U8 = mybir.dt.uint8
+FP8X4 = mybir.dt.float8_e4m3fn_x4
+FP4X4 = mybir.dt.float4_e2m1fn_x4
+ALU = mybir.AluOpType
+ACT = mybir.ActivationFunctionType
+
+D, T, I, Q, E, M = 512, 2048, 512, 256, 512, 1024
+P = 128
+PACK = 4
+BANK = 512
+QB = Q // P
+
+FLOPS = 2 * Q * T * D + 2 * E * Q * I
+
+
+def tile_attend_middle_bymember_lean_pl_kernel(
+    tc, query, keys_words, keys_scales, lam, slot_factor, vals, member, mgain, offs, offs2, offs3, offs4, out_0, out_1, out_2
+):
+    nc = tc.nc
+    with ExitStack() as ctx:
+        keep = ctx.enter_context(tc.tile_pool(name="keep", bufs=1))
+        psum = ctx.enter_context(tc.psum_pool(name="psum", bufs=1))
+
+        def sb(shape, dtype, name):
+            return keep.tile(shape, dtype, name=name, align_bytes=64)
+
+        def gather_v(out, window, offsets):
+            nc.vector.tensor_copy(out, window[:].indirect(offsets))
+
+        def gather_s(out, window, offsets):
+            nc.scalar.activation(out, window[:].indirect(offsets), ACT.Copy)
+
+        q_raw = sb([P, PACK, Q], F32, "q_raw")
+        k_words = sb([P, 2 * T], U8, "k_words")
+        k_scales = sb([P, T], U8, "k_scales")
+        lists = [keep.tile([P, I // 16], U16, name=f"list{n}") for n in range(3)]
+        list4 = keep.tile([P, Q // 16], U16, name="list4")
+        vals_sb = [sb([P, T], F32, f"vals{j}") for j in range(PACK)]
+        member_sb = [sb([P, M], F32, f"member{j}") for j in range(PACK)]
+        mgain_sb = sb([P, M], F32, "mgain_sb")
+        lam_sb = [sb([P, 1], F32, f"lam{b}") for b in range(QB)]
+        os_sb = sb([P, PACK], F32, "os_sb")
+        ident = sb([P, P], F32, "ident")
+
+        nc.vector.memset(k_scales[:].bitcast(I32), 0)
+        nc.sync.dma_start(q_raw[:], query.rearrange("(p j) q -> p j q", j=PACK))
+        for g in range(4):
+            nc.sync.dma_start(
+                k_scales[32 * g : 32 * g + 4, :].bitcast(I32), keys_scales[0, 4 * g : 4 * g + 4, :].bitcast(I32)
+            )
+        nc.sync.dma_start(k_words[:].bitcast(I32), keys_words[0].bitcast(I32))
+        vals_v = vals.rearrange("(p j) t -> p j t", j=PACK)
+        member_v = member.rearrange("(p j) m -> p j m", j=PACK)
+        nc.sync.dma_start(lists[0][:], offs)
+        nc.sync.dma_start(lists[1][:], offs2)
+        nc.sync.dma_start(vals_sb[0][:], vals_v[:, 0, :])
+        nc.sync.dma_start(lists[2][:], offs3)
+        for b in range(QB):
+            nc.sync.dma_start(lam_sb[b][:], lam[b * P : (b + 1) * P, :])
+        nc.sync.dma_start(os_sb[:], slot_factor.rearrange("o (p t) -> p (o t)", t=PACK))
+        nc.sync.dma_start(list4[:], offs4)
+        for j in range(1, PACK):
+            nc.sync.dma_start(vals_sb[j][:], vals_v[:, j, :])
+        nc.sync.dma_start(mgain_sb[:], mgain)
+        for j in range(PACK):
+            nc.sync.dma_start(member_sb[j][:], member_v[:, j, :])
+        make_identity(nc, ident[:])
+
+        q_bf = [sb([P, P, PACK], BF16, f"q_bf{b}") for b in range(QB)]
+        q_codes = [sb([P, P], U32, f"q_codes{b}") for b in range(QB)]
+        q_scales = [sb([P, P], U8, f"q_scales{b}") for b in range(QB)]
+        for b in range(QB):
+            nc.vector.tensor_copy(
+                q_bf[b][:].rearrange("p (c i) t -> p c t i", i=4),
+                q_raw[:, :, b * P : (b + 1) * P].rearrange("p t (c i) -> p c t i", i=4),
+            )
+        for b in range(QB):
+            nc.vector.quantize_mx(
+                out=q_codes[b][:].bitcast(FP8X4), scales=q_scales[b][:], in_=q_bf[b][:].rearrange("p q t -> p (q t)")
+            )
+
+        a_sb = [sb([P, T], F32, f"a{b}") for b in range(QB)]
+        for b in range(QB):
+            for c in range(T // BANK):
+                acc = psum.tile([P, BANK], F32, name="acc", tag="acc", bufs=4)
+                nc.tensor.matmul_mx(
+                    out=acc[:],
+                    lhsT=q_codes[b][:].bitcast(FP8X4),
+                    lhsT_scale=q_scales[b][:],
+                    rhs=k_words[:, 2 * c * BANK : 2 * (c + 1) * BANK].bitcast(FP4X4),
+                    rhs_scale=k_scales[:, c * BANK : (c + 1) * BANK],
+                    start=True,
+                    stop=True,
+                )
+                dst = a_sb[b][:, c * BANK : (c + 1) * BANK]
+                if b == 0 and c % 2 == 0:
+                    nc.vector.tensor_copy(dst, acc[:])
+                else:
+                    nc.scalar.copy(dst, acc[:])
+
+        picked = [[sb([P, I], F32, f"picked{b}_{n}") for n in range(3)] for b in range(QB)]
+        lo = [sb([P, I], F32, f"lo{b}") for b in range(QB)]
+        hi = [sb([P, I], F32, f"hi{b}") for b in range(QB)]
+        mid = [sb([P, I], F32, f"mid{b}") for b in range(QB)]
+        med = [sb([P, I], F32, f"med{b}") for b in range(QB)]
+        w_dealt = [sb([P, PACK, P], F32, f"w_dealt{b}") for b in range(QB)]
+        w_bf = sb([P, Q, PACK], BF16, "w_bf")
+        w_codes = sb([P, Q], U32, "w_codes")
+        w_scales = sb([P, Q], U8, "w_scales")
+        v_pick = [sb([P, I], BF16, f"v_pick{j}") for j in range(PACK)]
+        v_bf = [sb([P, P, PACK], BF16, f"v_bf{j}") for j in range(PACK)]
+        v_codes = [sb([P, P], U32, f"v_codes{j}") for j in range(PACK)]
+        v_scales = [sb([P, P], U8, f"v_scales{j}") for j in range(PACK)]
+        gain = sb([P, Q], F32, "gain")
+        m_pick = [sb([P, Q], F32, f"m_pick{j}") for j in range(PACK)]
+        scaled = [sb([P, Q], F32, f"scaled{j}") for j in range(PACK)]
+        y = sb([P, PACK, Q], F32, "y")
+        y_bf = sb([P, Q, PACK], BF16, "y_bf")
+        y_codes = sb([P, Q], U32, "y_codes")
+        y_scales = sb([P, Q], U8, "y_scales")
+
+        def low_high(b):
+            nc.vector.tensor_tensor(lo[b][:], picked[b][0][:], picked[b][1][:], ALU.min)
+            nc.vector.tensor_tensor(hi[b][:], picked[b][0][:], picked[b][1][:], ALU.max)
+
+        def median(b):
+            nc.vector.tensor_tensor(mid[b][:], hi[b][:], picked[b][2][:], ALU.min)
+            nc.vector.tensor_tensor(med[b][:], lo[b][:], mid[b][:], ALU.max)
+
+        def positive(b):
+            nc.scalar.activation(
+                w_dealt[b][:].rearrange("p t s -> p s t"),
+                med[b][:].rearrange("p (s t) -> p s t", t=PACK),
+                ACT.Relu,
+                scale=lam_sb[b][:],
+            )
+
+        def turn_weights(b):
+            turned = psum.tile([P, PACK, P], F32, name="turned_w", tag="late", bufs=2)
+            for t in range(PACK):
+                nc.tensor.transpose(turned[:, t, :], w_dealt[b][:, t, :], ident[:])
+            nc.vector.tensor_tensor(
+                w_bf[:, b * P : (b + 1) * P, :],
+                turned[:].rearrange("s t q -> s q t"),
+                os_sb[:].unsqueeze(1).to_broadcast([P, P, PACK]),
+                ALU.mult,
+            )
+
+        def turn_values(j):
+            words = v_pick[j][:].bitcast(F32)
+            turned = psum.tile([P, 2, P], F32, name="turned_v", tag="turned_v", bufs=2)
+            for u in range(2):
+                nc.tensor.transpose(turned[:, u, :], words[:, u : I // 2 : 2], ident[:])
+            nc.scalar.copy(
+                v_bf[j][:].rearrange("s e t -> s (e t)").bitcast(F32).rearrange("s (e u) -> s e u", u=2),
+                turned[:].rearrange("s u e -> s e u"),
+            )
+
+        def quantize_values(j):
+            nc.vector.quantize_mx(
+                out=v_codes[j][:].bitcast(FP8X4), scales=v_scales[j][:], in_=v_bf[j][:].rearrange("p e t -> p (e t)")
+            )
+
+        gather_v(picked[0][0][:], a_sb[0], lists[0][:])
+        gather_v(picked[0][1][:], a_sb[0], lists[1][:])
+        gather_s(picked[0][2][:], a_sb[0], lists[2][:])
+        low_high(0)
+        gather_s(picked[1][0][:], a_sb[1], lists[0][:])
+        gather_s(picked[1][1][:], a_sb[1], lists[1][:])
+        median(0)
+        gather_v(v_pick[0][:], vals_sb[0], lists[0][:])
+        positive(0)
+        gather_s(picked[1][2][:], a_sb[1], lists[2][:])
+        low_high(1)
+        turn_values(0)
+        turn_weights(0)
+        median(1)
+        gather_s(v_pick[1][:], vals_sb[1], lists[0][:])
+        positive(1)
+        gather_v(v_pick[2][:], vals_sb[2], lists[0][:])
+        turn_values(1)
+        gather_s(v_pick[3][:], vals_sb[3], lists[0][:])
+        turn_weights(1)
+        turn_values(2)
+        quantize_values(0)
+        quantize_values(1)
+        nc.vector.quantize_mx(
+            out=w_codes[:].bitcast(FP8X4), scales=w_scales[:], in_=w_bf[:].rearrange("p q t -> p (q t)")
+        )
+        gather_v(gain[:], mgain_sb, list4[:])
+        turn_values(3)
+        quantize_values(2)
+        quantize_values(3)
+
+        out_v = out_0.rearrange("(p j) q -> p j q", j=PACK)
+        for pair in range(2):
+            o_acc = psum.tile([P, 2, Q], F32, name="o_acc", tag="late", bufs=2)
+            for h in range(2):
+                j = 2 * pair + h
+                nc.tensor.matmul_mx(
+                    out=o_acc[:, h, :],
+                    lhsT=v_codes[j][:].bitcast(FP8X4),
+                    lhsT_scale=v_scales[j][:],
+                    rhs=w_codes[:].bitcast(FP8X4),
+                    rhs_scale=w_scales[:],
+                    start=True,
+                    stop=True,
+                )
+            for h in range(2):
+                j = 2 * pair + h
+                gather_s(m_pick[j][:], member_sb[j], list4[:])
+                nc.vector.tensor_tensor(scaled[j][:], o_acc[:, h, :], gain[:], ALU.mult)
+            for h in range(2):
+                j = 2 * pair + h
+                nc.vector.tensor_tensor(y[:, j, :], scaled[j][:], m_pick[j][:], ALU.add)
+                nc.sync.dma_start(out_v[:, j, :], y[:, j, :])
+
+        nc.vector.tensor_copy(
+            y_bf[:].rearrange("p (c i) t -> p c t i", i=4),
+            y[:].rearrange("p t (c i) -> p c t i", i=4),
+        )
+        nc.vector.quantize_mx(
+            out=y_codes[:].bitcast(FP8X4), scales=y_scales[:], in_=y_bf[:].rearrange("p q t -> p (q t)")
+        )
+        nc.sync.dma_start(out_1[0].rearrange("p c r -> p (c r)").bitcast(I32), y_codes[:].bitcast(I32))
+        for g in range(4):
+            nc.scalar.dma_start(
+                out_2[0, 4 * g : 4 * g + 4, :].bitcast(I32), y_scales[32 * g : 32 * g + 4, :].bitcast(I32)
+            )

@@ -19,6 +19,7 @@ P = 128
 PACK = 4
 BANK = 512
 QB = Q // P
+SPLIT = 160
 
 FLOPS = 2 * Q * T * D + 2 * E * Q * I
 
@@ -31,8 +32,8 @@ def tile_attend_middle_bymember_lean_pl_kernel(
         keep = ctx.enter_context(tc.tile_pool(name="keep", bufs=1))
         psum = ctx.enter_context(tc.psum_pool(name="psum", bufs=1))
 
-        def sb(shape, dtype, name):
-            return keep.tile(shape, dtype, name=name, align_bytes=64)
+        def sb(shape, dtype, name, tag=""):
+            return keep.tile(shape, dtype, name=name, tag=tag, align_bytes=64)
 
         def gather_v(out, window, offsets):
             nc.vector.tensor_copy(out, window[:].indirect(offsets))
@@ -40,41 +41,55 @@ def tile_attend_middle_bymember_lean_pl_kernel(
         def gather_s(out, window, offsets):
             nc.scalar.activation(out, window[:].indirect(offsets), ACT.Copy)
 
-        q_raw = sb([P, PACK, Q], F32, "q_raw")
-        k_words = sb([P, 2 * T], U8, "k_words")
+        def quantize(codes, scales, values):
+            nc.vector.quantize_mx(
+                out=codes[:].bitcast(FP8X4), scales=scales[:], in_=values[:].rearrange("p c t -> p (c t)")
+            )
+
+        q_raw = [sb([P, PACK, P], F32, f"q_raw{b}") for b in range(QB)]
+        k_words = [sb([P, T], U8, f"k_words{h}") for h in range(2)]
         k_scales = sb([P, T], U8, "k_scales")
         lists = [keep.tile([P, I // 16], U16, name=f"list{n}") for n in range(3)]
         list4 = keep.tile([P, Q // 16], U16, name="list4")
-        vals_sb = [sb([P, T], F32, f"vals{j}") for j in range(PACK)]
-        member_sb = [sb([P, M], F32, f"member{j}") for j in range(PACK)]
+        vals_sb = [sb([P, T], F32, f"vals{j}", tag=f"vals{j}") for j in range(PACK)]
+        member_sb = [sb([P, M], F32, f"member{j}", tag=f"member{j}") for j in range(PACK)]
         mgain_sb = sb([P, M], F32, "mgain_sb")
         lam_sb = [sb([P, 1], F32, f"lam{b}") for b in range(QB)]
         os_sb = sb([P, PACK], F32, "os_sb")
         ident = sb([P, P], F32, "ident")
+        banks = [psum.tile([P, BANK], F32, name=f"bank{n}") for n in range(8)]
 
-        nc.vector.memset(k_scales[:].bitcast(I32), 0)
-        nc.sync.dma_start(q_raw[:], query.rearrange("(p j) q -> p j q", j=PACK))
+        query_v = query.rearrange("(p j) q -> p j q", j=PACK)
+        vals_v = vals.rearrange("(p j) t -> p j t", j=PACK)
+        member_v = member.rearrange("(p j) m -> p j m", j=PACK)
+        out_v = out_0.rearrange("(p j) q -> p j q", j=PACK)
+
+        nc.gpsimd.memset(k_scales[:].bitcast(I32), 0)
+        make_identity(nc, ident[:])
+        nc.sync.dma_start(q_raw[0][:], query_v[:, :, 0:P])
         for g in range(4):
             nc.sync.dma_start(
                 k_scales[32 * g : 32 * g + 4, :].bitcast(I32), keys_scales[0, 4 * g : 4 * g + 4, :].bitcast(I32)
             )
-        nc.sync.dma_start(k_words[:].bitcast(I32), keys_words[0].bitcast(I32))
-        vals_v = vals.rearrange("(p j) t -> p j t", j=PACK)
-        member_v = member.rearrange("(p j) m -> p j m", j=PACK)
+        nc.sync.dma_start(k_words[0][:].bitcast(I32), keys_words[0, :, 0:T].bitcast(I32))
+        nc.sync.dma_start(q_raw[1][:], query_v[:, :, P : 2 * P])
+        nc.sync.dma_start(k_words[1][:].bitcast(I32), keys_words[0, :, T : 2 * T].bitcast(I32))
+        nc.sync.dma_start(list4[:], offs4)
+        nc.vector.memset(mgain_sb[:], 0.0)
+        nc.sync.dma_start(mgain_sb[0:1, :], mgain[0:1, :])
         nc.sync.dma_start(lists[0][:], offs)
         nc.sync.dma_start(lists[1][:], offs2)
-        nc.sync.dma_start(vals_sb[0][:], vals_v[:, 0, :])
         nc.sync.dma_start(lists[2][:], offs3)
+        nc.sync.dma_start(vals_sb[0][:], vals_v[:, 0, :])
         for b in range(QB):
             nc.sync.dma_start(lam_sb[b][:], lam[b * P : (b + 1) * P, :])
         nc.sync.dma_start(os_sb[:], slot_factor.rearrange("o (p t) -> p (o t)", t=PACK))
-        nc.sync.dma_start(list4[:], offs4)
         for j in range(1, PACK):
             nc.sync.dma_start(vals_sb[j][:], vals_v[:, j, :])
-        nc.sync.dma_start(mgain_sb[:], mgain)
         for j in range(PACK):
             nc.sync.dma_start(member_sb[j][:], member_v[:, j, :])
-        make_identity(nc, ident[:])
+
+        gain_row = sb([P, Q], F32, "gain_row")
 
         q_bf = [sb([P, P, PACK], BF16, f"q_bf{b}") for b in range(QB)]
         q_codes = [sb([P, P], U32, f"q_codes{b}") for b in range(QB)]
@@ -82,156 +97,148 @@ def tile_attend_middle_bymember_lean_pl_kernel(
         for b in range(QB):
             nc.vector.tensor_copy(
                 q_bf[b][:].rearrange("p (c i) t -> p c t i", i=4),
-                q_raw[:, :, b * P : (b + 1) * P].rearrange("p t (c i) -> p c t i", i=4),
+                q_raw[b][:].rearrange("p t (c i) -> p c t i", i=4),
             )
-        for b in range(QB):
-            nc.vector.quantize_mx(
-                out=q_codes[b][:].bitcast(FP8X4), scales=q_scales[b][:], in_=q_bf[b][:].rearrange("p q t -> p (q t)")
-            )
+            quantize(q_codes[b], q_scales[b], q_bf[b])
 
-        a_sb = [sb([P, T], F32, f"a{b}") for b in range(QB)]
+        a_sb = [sb([P, T], F32, f"a{b}", tag=f"a{b}") for b in range(QB)]
         for b in range(QB):
             for c in range(T // BANK):
-                acc = psum.tile([P, BANK], F32, name="acc", tag="acc", bufs=4)
+                acc = banks[4 * b + c]
                 nc.tensor.matmul_mx(
                     out=acc[:],
                     lhsT=q_codes[b][:].bitcast(FP8X4),
                     lhsT_scale=q_scales[b][:],
-                    rhs=k_words[:, 2 * c * BANK : 2 * (c + 1) * BANK].bitcast(FP4X4),
+                    rhs=k_words[c // 2][:, 2 * (c % 2) * BANK : 2 * (c % 2 + 1) * BANK].bitcast(FP4X4),
                     rhs_scale=k_scales[:, c * BANK : (c + 1) * BANK],
                     start=True,
                     stop=True,
                 )
                 dst = a_sb[b][:, c * BANK : (c + 1) * BANK]
-                if b == 0 and c % 2 == 0:
-                    nc.vector.tensor_copy(dst, acc[:])
-                else:
+                if b == 0 and c % 2 == 1:
                     nc.scalar.copy(dst, acc[:])
+                else:
+                    nc.vector.tensor_copy(dst, acc[:])
 
         picked = [[sb([P, I], F32, f"picked{b}_{n}") for n in range(3)] for b in range(QB)]
-        lo = [sb([P, I], F32, f"lo{b}") for b in range(QB)]
-        hi = [sb([P, I], F32, f"hi{b}") for b in range(QB)]
-        mid = [sb([P, I], F32, f"mid{b}") for b in range(QB)]
-        med = [sb([P, I], F32, f"med{b}") for b in range(QB)]
+        ring = [sb([P, I], F32, f"ring{n}", tag=f"ring{n}") for n in range(4)]
         w_dealt = [sb([P, PACK, P], F32, f"w_dealt{b}") for b in range(QB)]
         w_bf = sb([P, Q, PACK], BF16, "w_bf")
-        w_codes = sb([P, Q], U32, "w_codes")
         w_scales = sb([P, Q], U8, "w_scales")
-        v_pick = [sb([P, I], BF16, f"v_pick{j}") for j in range(PACK)]
-        v_bf = [sb([P, P, PACK], BF16, f"v_bf{j}") for j in range(PACK)]
-        v_codes = [sb([P, P], U32, f"v_codes{j}") for j in range(PACK)]
-        v_scales = [sb([P, P], U8, f"v_scales{j}") for j in range(PACK)]
+        v_codes = [sb([P, 2 * P], U32, f"v_codes{h}") for h in range(2)]
+        v_scales = [sb([P, 2 * P], U8, f"v_scales{h}") for h in range(2)]
         gain = sb([P, Q], F32, "gain")
-        m_pick = [sb([P, Q], F32, f"m_pick{j}") for j in range(PACK)]
-        scaled = [sb([P, Q], F32, f"scaled{j}") for j in range(PACK)]
+        m_pick = [sb([P, 2, Q], F32, f"m_pick{h}") for h in range(2)]
         y = sb([P, PACK, Q], F32, "y")
-        y_bf = sb([P, Q, PACK], BF16, "y_bf")
         y_codes = sb([P, Q], U32, "y_codes")
         y_scales = sb([P, Q], U8, "y_scales")
 
         def low_high(b):
-            nc.vector.tensor_tensor(lo[b][:], picked[b][0][:], picked[b][1][:], ALU.min)
-            nc.vector.tensor_tensor(hi[b][:], picked[b][0][:], picked[b][1][:], ALU.max)
+            lo, hi = ring[3 * b % 4], ring[(3 * b + 1) % 4]
+            nc.vector.tensor_tensor(hi[:], picked[b][0][:], picked[b][1][:], ALU.max)
+            nc.vector.tensor_tensor(lo[:], picked[b][0][:], picked[b][1][:], ALU.min)
 
         def median(b):
-            nc.vector.tensor_tensor(mid[b][:], hi[b][:], picked[b][2][:], ALU.min)
-            nc.vector.tensor_tensor(med[b][:], lo[b][:], mid[b][:], ALU.max)
-
-        def positive(b):
-            nc.scalar.activation(
-                w_dealt[b][:].rearrange("p t s -> p s t"),
-                med[b][:].rearrange("p (s t) -> p s t", t=PACK),
-                ACT.Relu,
-                scale=lam_sb[b][:],
-            )
+            lo, hi, mid, med = (ring[(3 * b + n) % 4] for n in range(4))
+            halves = (slice(0, I // 2), slice(I // 2, I))
+            for c in halves:
+                nc.vector.tensor_tensor(mid[:, c], hi[:, c], picked[b][2][:, c], ALU.min)
+            for c in halves:
+                nc.vector.tensor_tensor(med[:, c], lo[:, c], mid[:, c], ALU.max)
+            for n, c in enumerate(halves):
+                nc.vector.tensor_scalar(
+                    w_dealt[b][:, :, n * P // 2 : (n + 1) * P // 2].rearrange("p t s -> p s t"),
+                    med[:, c].rearrange("p (s t) -> p s t", t=PACK),
+                    lam_sb[b][:],
+                    0.0,
+                    ALU.mult,
+                    ALU.max,
+                )
 
         def turn_weights(b):
-            turned = psum.tile([P, PACK, P], F32, name="turned_w", tag="late", bufs=2)
+            turned = banks[b][:].rearrange("s (t q) -> s t q", t=PACK)
             for t in range(PACK):
                 nc.tensor.transpose(turned[:, t, :], w_dealt[b][:, t, :], ident[:])
             nc.vector.tensor_tensor(
                 w_bf[:, b * P : (b + 1) * P, :],
-                turned[:].rearrange("s t q -> s q t"),
+                turned.rearrange("s t q -> s q t"),
                 os_sb[:].unsqueeze(1).to_broadcast([P, P, PACK]),
                 ALU.mult,
             )
 
-        def turn_values(j):
-            words = v_pick[j][:].bitcast(F32)
-            turned = psum.tile([P, 2, P], F32, name="turned_v", tag="turned_v", bufs=2)
-            for u in range(2):
-                nc.tensor.transpose(turned[:, u, :], words[:, u : I // 2 : 2], ident[:])
-            nc.scalar.copy(
-                v_bf[j][:].rearrange("s e t -> s (e t)").bitcast(F32).rearrange("s (e u) -> s e u", u=2),
-                turned[:].rearrange("s u e -> s e u"),
+        def turn_values(bank, v_pick, v_bf, copy):
+            turned = bank[:].rearrange("s (g u e) -> s g u e", g=2, u=2)
+            for g in range(2):
+                words = v_pick[:, g, :].bitcast(F32)
+                for u in range(2):
+                    nc.tensor.transpose(turned[:, g, u, :], words[:, u : I // 2 : 2], ident[:])
+            copy(
+                v_bf[:].rearrange("s c t -> s (c t)").bitcast(F32).rearrange("s (g e u) -> s g e u", g=2, u=2),
+                turned.rearrange("s g u e -> s g e u"),
             )
 
-        def quantize_values(j):
-            nc.vector.quantize_mx(
-                out=v_codes[j][:].bitcast(FP8X4), scales=v_scales[j][:], in_=v_bf[j][:].rearrange("p e t -> p (e t)")
+        for n in range(3):
+            gather_s(picked[0][n][:], a_sb[0], lists[n][:])
+        for n in range(2):
+            gather_s(picked[1][n][:], a_sb[1], lists[n][:])
+        gather_v(gain_row[:], mgain_sb, list4[:])
+        gain_col = sb([P, QB], F32, "gain_col")
+        down = banks[7][:, 0:Q].rearrange("q (b r) -> q b r", b=QB)
+        for b in range(QB):
+            nc.tensor.transpose(down[:, b, :], gain_row[:, b * P : (b + 1) * P], ident[:])
+        nc.vector.tensor_copy(gain_col[:], down[:, :, 0])
+        for b in range(QB):
+            nc.tensor.transpose(
+                banks[6][:, b * P : (b + 1) * P], gain_col[:, b : b + 1].to_broadcast([P, P]), ident[:]
             )
-
-        gather_v(picked[0][0][:], a_sb[0], lists[0][:])
-        gather_v(picked[0][1][:], a_sb[0], lists[1][:])
-        gather_s(picked[0][2][:], a_sb[0], lists[2][:])
+        nc.vector.tensor_copy(gain[:], banks[6][:, 0:Q])
+        gather_v(picked[1][2][:], a_sb[1], lists[2][:])
         low_high(0)
-        gather_s(picked[1][0][:], a_sb[1], lists[0][:])
-        gather_s(picked[1][1][:], a_sb[1], lists[1][:])
         median(0)
-        gather_v(v_pick[0][:], vals_sb[0], lists[0][:])
-        positive(0)
-        gather_s(picked[1][2][:], a_sb[1], lists[2][:])
         low_high(1)
-        turn_values(0)
         turn_weights(0)
         median(1)
-        gather_s(v_pick[1][:], vals_sb[1], lists[0][:])
-        positive(1)
-        gather_v(v_pick[2][:], vals_sb[2], lists[0][:])
-        turn_values(1)
-        gather_s(v_pick[3][:], vals_sb[3], lists[0][:])
+        v_pick = [sb([P, 2, I], BF16, "v_pick0", tag="a1"), sb([P, 2, I], BF16, "v_pick1")]
+        for j in range(PACK):
+            gather_s(v_pick[j // 2][:, j % 2, :], vals_sb[j], lists[0][:])
+        v_bf = [sb([P, 2 * P, PACK], BF16, "v_bf0", tag="ring2")]
+        turn_values(banks[0], v_pick[0], v_bf[0], nc.vector.tensor_copy)
         turn_weights(1)
-        turn_values(2)
-        quantize_values(0)
-        quantize_values(1)
-        nc.vector.quantize_mx(
-            out=w_codes[:].bitcast(FP8X4), scales=w_scales[:], in_=w_bf[:].rearrange("p q t -> p (q t)")
-        )
-        gather_v(gain[:], mgain_sb, list4[:])
-        turn_values(3)
-        quantize_values(2)
-        quantize_values(3)
+        quantize(v_codes[0], v_scales[0], v_bf[0])
+        w_codes = sb([P, Q], U32, "w_codes", tag="vals3")
+        quantize(w_codes, w_scales, w_bf)
+        gather_s(m_pick[0][:, 0, :], member_sb[0], list4[:])
+        v_bf.append(sb([P, 2 * P, PACK], BF16, "v_bf1", tag="member0"))
+        turn_values(banks[2], v_pick[1], v_bf[1], nc.scalar.copy)
+        for j in range(1, PACK):
+            gather_s(m_pick[j // 2][:, j % 2, :], member_sb[j], list4[:])
+        y_bf = sb([P, Q, PACK], BF16, "y_bf")
+        quantize(v_codes[1], v_scales[1], v_bf[1])
+        scaled = [sb([P, 2, Q], F32, "scaled0", tag="member0"), sb([P, 2, Q], F32, "scaled1")]
 
-        out_v = out_0.rearrange("(p j) q -> p j q", j=PACK)
-        for pair in range(2):
-            o_acc = psum.tile([P, 2, Q], F32, name="o_acc", tag="late", bufs=2)
-            for h in range(2):
-                j = 2 * pair + h
+        for h in range(2):
+            o_acc = banks[4 + h][:].rearrange("p (g q) -> p g q", g=2)
+            for g in range(2):
                 nc.tensor.matmul_mx(
-                    out=o_acc[:, h, :],
-                    lhsT=v_codes[j][:].bitcast(FP8X4),
-                    lhsT_scale=v_scales[j][:],
+                    out=o_acc[:, g, :],
+                    lhsT=v_codes[h][:, g * P : (g + 1) * P].bitcast(FP8X4),
+                    lhsT_scale=v_scales[h][:, g * P : (g + 1) * P],
                     rhs=w_codes[:].bitcast(FP8X4),
                     rhs_scale=w_scales[:],
                     start=True,
                     stop=True,
                 )
-            for h in range(2):
-                j = 2 * pair + h
-                gather_s(m_pick[j][:], member_sb[j], list4[:])
-                nc.vector.tensor_tensor(scaled[j][:], o_acc[:, h, :], gain[:], ALU.mult)
-            for h in range(2):
-                j = 2 * pair + h
-                nc.vector.tensor_tensor(y[:, j, :], scaled[j][:], m_pick[j][:], ALU.add)
-                nc.sync.dma_start(out_v[:, j, :], y[:, j, :])
+            nc.vector.tensor_tensor(scaled[h][:], o_acc, gain[:].unsqueeze(1).to_broadcast([P, 2, Q]), ALU.mult)
+        for h in range(2):
+            nc.vector.tensor_tensor(y[:, 2 * h : 2 * h + 2, :], scaled[h][:], m_pick[h][:], ALU.add)
+            nc.sync.dma_start(out_v[:, 2 * h : 2 * h + 2, :], y[:, 2 * h : 2 * h + 2, :])
+        for copy, c in ((nc.vector.tensor_copy, slice(0, SPLIT)), (nc.scalar.copy, slice(SPLIT, Q))):
+            copy(
+                y_bf[:, c, :].rearrange("p (c i) t -> p c t i", i=4),
+                y[:, :, c].rearrange("p t (c i) -> p c t i", i=4),
+            )
 
-        nc.vector.tensor_copy(
-            y_bf[:].rearrange("p (c i) t -> p c t i", i=4),
-            y[:].rearrange("p t (c i) -> p c t i", i=4),
-        )
-        nc.vector.quantize_mx(
-            out=y_codes[:].bitcast(FP8X4), scales=y_scales[:], in_=y_bf[:].rearrange("p q t -> p (q t)")
-        )
+        quantize(y_codes, y_scales, y_bf)
         nc.sync.dma_start(out_1[0].rearrange("p c r -> p (c r)").bitcast(I32), y_codes[:].bitcast(I32))
         for g in range(4):
             nc.scalar.dma_start(

@@ -19,7 +19,11 @@ P = 128
 PACK = 4
 BANK = 512
 QB = Q // P
-SPLIT = 160
+QUADRANTS = 4
+GROUP = 16
+RING = 4
+RUN = 4
+Y_VECTOR_COLUMNS = 160
 
 FLOPS = 2 * Q * T * D + 2 * E * Q * I
 
@@ -35,10 +39,10 @@ def tile_attend_middle_bymember_lean_pl_kernel(
         def sb(shape, dtype, name, tag=""):
             return keep.tile(shape, dtype, name=name, tag=tag, align_bytes=64)
 
-        def gather_v(out, window, offsets):
+        def gather_on_vector(out, window, offsets):
             nc.vector.tensor_copy(out, window[:].indirect(offsets))
 
-        def gather_s(out, window, offsets):
+        def gather_on_scalar(out, window, offsets):
             nc.scalar.activation(out, window[:].indirect(offsets), ACT.Copy)
 
         def quantize(codes, scales, values):
@@ -46,11 +50,17 @@ def tile_attend_middle_bymember_lean_pl_kernel(
                 out=codes[:].bitcast(FP8X4), scales=scales[:], in_=values[:].rearrange("p c t -> p (c t)")
             )
 
+        def interleave(copy, values, planes):
+            copy(
+                values.rearrange("p (c i) t -> p c t i", i=RUN),
+                planes.rearrange("p t (c i) -> p c t i", i=RUN),
+            )
+
         q_raw = [sb([P, PACK, P], F32, f"q_raw{b}") for b in range(QB)]
         k_words = [sb([P, T], U8, f"k_words{h}") for h in range(2)]
         k_scales = sb([P, T], U8, "k_scales")
-        lists = [keep.tile([P, I // 16], U16, name=f"list{n}") for n in range(3)]
-        list4 = keep.tile([P, Q // 16], U16, name="list4")
+        lists = [keep.tile([P, I // GROUP], U16, name=f"list{n}") for n in range(3)]
+        list4 = keep.tile([P, Q // GROUP], U16, name="list4")
         vals_sb = [sb([P, T], F32, f"vals{j}", tag=f"vals{j}") for j in range(PACK)]
         member_sb = [sb([P, M], F32, f"member{j}", tag=f"member{j}") for j in range(PACK)]
         mgain_sb = sb([P, M], F32, "mgain_sb")
@@ -67,9 +77,10 @@ def tile_attend_middle_bymember_lean_pl_kernel(
         nc.gpsimd.memset(k_scales[:].bitcast(I32), 0)
         make_identity(nc, ident[:])
         nc.sync.dma_start(q_raw[0][:], query_v[:, :, 0:P])
-        for g in range(4):
+        for quad in range(QUADRANTS):
             nc.sync.dma_start(
-                k_scales[32 * g : 32 * g + 4, :].bitcast(I32), keys_scales[0, 4 * g : 4 * g + 4, :].bitcast(I32)
+                k_scales[32 * quad : 32 * quad + 4, :].bitcast(I32),
+                keys_scales[0, 4 * quad : 4 * quad + 4, :].bitcast(I32),
             )
         nc.sync.dma_start(k_words[0][:].bitcast(I32), keys_words[0, :, 0:T].bitcast(I32))
         nc.sync.dma_start(q_raw[1][:], query_v[:, :, P : 2 * P])
@@ -81,65 +92,71 @@ def tile_attend_middle_bymember_lean_pl_kernel(
         nc.sync.dma_start(lists[1][:], offs2)
         nc.sync.dma_start(lists[2][:], offs3)
         nc.sync.dma_start(vals_sb[0][:], vals_v[:, 0, :])
-        for b in range(QB):
-            nc.sync.dma_start(lam_sb[b][:], lam[b * P : (b + 1) * P, :])
+        nc.sync.dma_start(lam_sb[0][:], lam[0:P, :])
+        nc.sync.dma_start(vals_sb[1][:], vals_v[:, 1, :])
         nc.sync.dma_start(os_sb[:], slot_factor.rearrange("o (p t) -> p (o t)", t=PACK))
-        for j in range(1, PACK):
+        nc.sync.dma_start(lam_sb[1][:], lam[P : 2 * P, :])
+        for j in range(2, PACK):
             nc.sync.dma_start(vals_sb[j][:], vals_v[:, j, :])
         for j in range(PACK):
             nc.sync.dma_start(member_sb[j][:], member_v[:, j, :])
 
         gain_row = sb([P, Q], F32, "gain_row")
+        gather_on_scalar(gain_row[:], mgain_sb, list4[:])
 
         q_bf = [sb([P, P, PACK], BF16, f"q_bf{b}") for b in range(QB)]
         q_codes = [sb([P, P], U32, f"q_codes{b}") for b in range(QB)]
         q_scales = [sb([P, P], U8, f"q_scales{b}") for b in range(QB)]
         for b in range(QB):
-            nc.vector.tensor_copy(
-                q_bf[b][:].rearrange("p (c i) t -> p c t i", i=4),
-                q_raw[b][:].rearrange("p t (c i) -> p c t i", i=4),
-            )
+            interleave(nc.vector.tensor_copy, q_bf[b][:], q_raw[b][:])
             quantize(q_codes[b], q_scales[b], q_bf[b])
 
         a_sb = [sb([P, T], F32, f"a{b}", tag=f"a{b}") for b in range(QB)]
-        for b in range(QB):
-            for c in range(T // BANK):
-                acc = banks[4 * b + c]
-                nc.tensor.matmul_mx(
-                    out=acc[:],
-                    lhsT=q_codes[b][:].bitcast(FP8X4),
-                    lhsT_scale=q_scales[b][:],
-                    rhs=k_words[c // 2][:, 2 * (c % 2) * BANK : 2 * (c % 2 + 1) * BANK].bitcast(FP4X4),
-                    rhs_scale=k_scales[:, c * BANK : (c + 1) * BANK],
-                    start=True,
-                    stop=True,
-                )
-                dst = a_sb[b][:, c * BANK : (c + 1) * BANK]
-                if b == 0 and c % 2 == 1:
-                    nc.scalar.copy(dst, acc[:])
-                else:
-                    nc.vector.tensor_copy(dst, acc[:])
+
+        def scores(b, first, width, bank, copy):
+            acc = bank[:, 0:width]
+            half, byte = divmod(2 * first, T)
+            nc.tensor.matmul_mx(
+                out=acc,
+                lhsT=q_codes[b][:].bitcast(FP8X4),
+                lhsT_scale=q_scales[b][:],
+                rhs=k_words[half][:, byte : byte + 2 * width].bitcast(FP4X4),
+                rhs_scale=k_scales[:, first : first + width],
+                start=True,
+                stop=True,
+            )
+            copy(a_sb[b][:, first : first + width], acc)
+
+        widths = (BANK, BANK, BANK, BANK // 2, BANK // 2)
+        for n, width in enumerate(widths):
+            copy = nc.scalar.copy if n % 2 else nc.vector.tensor_copy
+            scores(0, sum(widths[:n]), width, banks[n], copy)
+        for c in range(T // BANK):
+            scores(1, c * BANK, BANK, banks[(len(widths) + c) % len(banks)], nc.vector.tensor_copy)
 
         picked = [[sb([P, I], F32, f"picked{b}_{n}") for n in range(3)] for b in range(QB)]
-        ring = [sb([P, I], F32, f"ring{n}", tag=f"ring{n}") for n in range(4)]
+        ring = [sb([P, I], F32, f"ring{n}", tag=f"ring{n}") for n in range(RING)]
         w_dealt = [sb([P, PACK, P], F32, f"w_dealt{b}") for b in range(QB)]
         w_bf = sb([P, Q, PACK], BF16, "w_bf")
         w_scales = sb([P, Q], U8, "w_scales")
         v_codes = [sb([P, 2 * P], U32, f"v_codes{h}") for h in range(2)]
         v_scales = [sb([P, 2 * P], U8, f"v_scales{h}") for h in range(2)]
         gain = sb([P, Q], F32, "gain")
-        m_pick = [sb([P, 2, Q], F32, f"m_pick{h}") for h in range(2)]
+        m_pick = [sb([P, 2, Q], F32, "m_pick0")]
         y = sb([P, PACK, Q], F32, "y")
         y_codes = sb([P, Q], U32, "y_codes")
         y_scales = sb([P, Q], U8, "y_scales")
 
+        def ring_tiles(b):
+            return [ring[(n - b) % RING] for n in range(RING)]
+
         def low_high(b):
-            lo, hi = ring[3 * b % 4], ring[(3 * b + 1) % 4]
+            lo, hi = ring_tiles(b)[:2]
             nc.vector.tensor_tensor(hi[:], picked[b][0][:], picked[b][1][:], ALU.max)
             nc.vector.tensor_tensor(lo[:], picked[b][0][:], picked[b][1][:], ALU.min)
 
-        def median(b):
-            lo, hi, mid, med = (ring[(3 * b + n) % 4] for n in range(4))
+        def weights(b):
+            lo, hi, mid, med = ring_tiles(b)
             halves = (slice(0, I // 2), slice(I // 2, I))
             for c in halves:
                 nc.vector.tensor_tensor(mid[:, c], hi[:, c], picked[b][2][:, c], ALU.min)
@@ -166,56 +183,59 @@ def tile_attend_middle_bymember_lean_pl_kernel(
                 ALU.mult,
             )
 
-        def turn_values(bank, v_pick, v_bf, copy):
+        def turn_values(bank, picked_pair, turned_pair, copy):
             turned = bank[:].rearrange("s (g u e) -> s g u e", g=2, u=2)
             for g in range(2):
-                words = v_pick[:, g, :].bitcast(F32)
+                words = picked_pair[:, g, :].bitcast(F32)
                 for u in range(2):
                     nc.tensor.transpose(turned[:, g, u, :], words[:, u : I // 2 : 2], ident[:])
             copy(
-                v_bf[:].rearrange("s c t -> s (c t)").bitcast(F32).rearrange("s (g e u) -> s g e u", g=2, u=2),
+                turned_pair[:].rearrange("s c t -> s (c t)").bitcast(F32).rearrange("s (g e u) -> s g e u", g=2, u=2),
                 turned.rearrange("s g u e -> s g e u"),
             )
 
         for n in range(3):
-            gather_s(picked[0][n][:], a_sb[0], lists[n][:])
+            gather_on_scalar(picked[0][n][:], a_sb[0], lists[n][:])
         for n in range(2):
-            gather_s(picked[1][n][:], a_sb[1], lists[n][:])
-        gather_v(gain_row[:], mgain_sb, list4[:])
+            gather_on_scalar(picked[1][n][:], a_sb[1], lists[n][:])
+
         gain_col = sb([P, QB], F32, "gain_col")
-        down = banks[7][:, 0:Q].rearrange("q (b r) -> q b r", b=QB)
+        down = banks[3][:, 0:Q].rearrange("q (b r) -> q b r", b=QB)
         for b in range(QB):
             nc.tensor.transpose(down[:, b, :], gain_row[:, b * P : (b + 1) * P], ident[:])
         nc.vector.tensor_copy(gain_col[:], down[:, :, 0])
         for b in range(QB):
             nc.tensor.transpose(
-                banks[6][:, b * P : (b + 1) * P], gain_col[:, b : b + 1].to_broadcast([P, P]), ident[:]
+                banks[4][:, b * P : (b + 1) * P], gain_col[:, b : b + 1].to_broadcast([P, P]), ident[:]
             )
-        nc.vector.tensor_copy(gain[:], banks[6][:, 0:Q])
-        gather_v(picked[1][2][:], a_sb[1], lists[2][:])
+        nc.vector.tensor_copy(gain[:], banks[4][:, 0:Q])
+
+        gather_on_vector(picked[1][2][:], a_sb[1], lists[2][:])
         low_high(0)
-        median(0)
+        weights(0)
         low_high(1)
         turn_weights(0)
-        median(1)
-        v_pick = [sb([P, 2, I], BF16, "v_pick0", tag="a1"), sb([P, 2, I], BF16, "v_pick1")]
+        weights(1)
+
+        v_pick = [sb([P, 2, I], BF16, "v_pick0", tag="a1"), sb([P, 2, I], BF16, "v_pick1", tag="last_pick")]
         for j in range(PACK):
-            gather_s(v_pick[j // 2][:, j % 2, :], vals_sb[j], lists[0][:])
+            gather_on_scalar(v_pick[j // 2][:, j % 2, :], vals_sb[j], lists[0][:])
         v_bf = [sb([P, 2 * P, PACK], BF16, "v_bf0", tag="ring2")]
         turn_values(banks[0], v_pick[0], v_bf[0], nc.vector.tensor_copy)
         turn_weights(1)
         quantize(v_codes[0], v_scales[0], v_bf[0])
         w_codes = sb([P, Q], U32, "w_codes", tag="vals3")
         quantize(w_codes, w_scales, w_bf)
-        gather_s(m_pick[0][:, 0, :], member_sb[0], list4[:])
+        gather_on_scalar(m_pick[0][:, 0, :], member_sb[0], list4[:])
         v_bf.append(sb([P, 2 * P, PACK], BF16, "v_bf1", tag="member0"))
         turn_values(banks[2], v_pick[1], v_bf[1], nc.scalar.copy)
+        m_pick.append(sb([P, 2, Q], F32, "m_pick1", tag="last_pick"))
         for j in range(1, PACK):
-            gather_s(m_pick[j // 2][:, j % 2, :], member_sb[j], list4[:])
+            gather_on_scalar(m_pick[j // 2][:, j % 2, :], member_sb[j], list4[:])
         y_bf = sb([P, Q, PACK], BF16, "y_bf")
         quantize(v_codes[1], v_scales[1], v_bf[1])
-        scaled = [sb([P, 2, Q], F32, "scaled0", tag="member0"), sb([P, 2, Q], F32, "scaled1")]
 
+        scaled = [sb([P, 2, Q], F32, "scaled0", tag="member0"), sb([P, 2, Q], F32, "scaled1")]
         for h in range(2):
             o_acc = banks[4 + h][:].rearrange("p (g q) -> p g q", g=2)
             for g in range(2):
@@ -232,15 +252,16 @@ def tile_attend_middle_bymember_lean_pl_kernel(
         for h in range(2):
             nc.vector.tensor_tensor(y[:, 2 * h : 2 * h + 2, :], scaled[h][:], m_pick[h][:], ALU.add)
             nc.sync.dma_start(out_v[:, 2 * h : 2 * h + 2, :], y[:, 2 * h : 2 * h + 2, :])
-        for copy, c in ((nc.vector.tensor_copy, slice(0, SPLIT)), (nc.scalar.copy, slice(SPLIT, Q))):
-            copy(
-                y_bf[:, c, :].rearrange("p (c i) t -> p c t i", i=4),
-                y[:, :, c].rearrange("p t (c i) -> p c t i", i=4),
-            )
 
+        for copy, c in (
+            (nc.vector.tensor_copy, slice(0, Y_VECTOR_COLUMNS)),
+            (nc.scalar.copy, slice(Y_VECTOR_COLUMNS, Q)),
+        ):
+            interleave(copy, y_bf[:, c, :], y[:, :, c])
         quantize(y_codes, y_scales, y_bf)
         nc.sync.dma_start(out_1[0].rearrange("p c r -> p (c r)").bitcast(I32), y_codes[:].bitcast(I32))
-        for g in range(4):
+        for quad in range(QUADRANTS):
             nc.scalar.dma_start(
-                out_2[0, 4 * g : 4 * g + 4, :].bitcast(I32), y_scales[32 * g : 32 * g + 4, :].bitcast(I32)
+                out_2[0, 4 * quad : 4 * quad + 4, :].bitcast(I32),
+                y_scales[32 * quad : 32 * quad + 4, :].bitcast(I32),
             )

from contextlib import ExitStack

import concourse.mybir as mybir
from concourse.masks import make_identity

F32 = mybir.dt.float32
BF16 = mybir.dt.bfloat16
I32 = mybir.dt.int32
U32 = mybir.dt.uint32
U16 = mybir.dt.uint16
U8 = mybir.dt.uint8
FP8X4 = mybir.dt.float8_e4m3fn_x4
FP4X4 = mybir.dt.float4_e2m1fn_x4
ALU = mybir.AluOpType
ACT = mybir.ActivationFunctionType

D, T, I, Q, E, M = 512, 2048, 512, 256, 512, 1024
P = 128
PACK = 4
BANK = 512
QB = Q // P
QUADRANTS = 4
GROUP = 16
RING = 4
RUN = 4
Y_VECTOR_COLUMNS = 160

FLOPS = 2 * Q * T * D + 2 * E * Q * I


def tile_attend_middle_bymember_lean_pl_kernel(
    tc, query, keys_words, keys_scales, lam, slot_factor, vals, member, mgain, offs, offs2, offs3, offs4, out_0, out_1, out_2
):
    nc = tc.nc
    with ExitStack() as ctx:
        keep = ctx.enter_context(tc.tile_pool(name="keep", bufs=1))
        psum = ctx.enter_context(tc.psum_pool(name="psum", bufs=1))

        def sb(shape, dtype, name, tag=""):
            return keep.tile(shape, dtype, name=name, tag=tag, align_bytes=64)

        def gather_on_vector(out, window, offsets):
            nc.vector.tensor_copy(out, window[:].indirect(offsets))

        def gather_on_scalar(out, window, offsets):
            nc.scalar.activation(out, window[:].indirect(offsets), ACT.Copy)

        def quantize(codes, scales, values):
            nc.vector.quantize_mx(
                out=codes[:].bitcast(FP8X4), scales=scales[:], in_=values[:].rearrange("p c t -> p (c t)")
            )

        def interleave(copy, values, planes):
            copy(
                values.rearrange("p (c i) t -> p c t i", i=RUN),
                planes.rearrange("p t (c i) -> p c t i", i=RUN),
            )

        q_raw = [sb([P, PACK, P], F32, f"q_raw{b}") for b in range(QB)]
        k_words = [sb([P, T], U8, f"k_words{h}") for h in range(2)]
        k_scales = sb([P, T], U8, "k_scales")
        lists = [keep.tile([P, I // GROUP], U16, name=f"list{n}") for n in range(3)]
        list4 = keep.tile([P, Q // GROUP], U16, name="list4")
        vals_sb = [sb([P, T], F32, f"vals{j}", tag=f"vals{j}") for j in range(PACK)]
        member_sb = [sb([P, M], F32, f"member{j}", tag=f"member{j}") for j in range(PACK)]
        mgain_sb = sb([P, M], F32, "mgain_sb")
        lam_sb = [sb([P, 1], F32, f"lam{b}") for b in range(QB)]
        os_sb = sb([P, PACK], F32, "os_sb")
        ident = sb([P, P], F32, "ident")
        banks = [psum.tile([P, BANK], F32, name=f"bank{n}") for n in range(8)]

        query_v = query.rearrange("(p j) q -> p j q", j=PACK)
        vals_v = vals.rearrange("(p j) t -> p j t", j=PACK)
        member_v = member.rearrange("(p j) m -> p j m", j=PACK)
        out_v = out_0.rearrange("(p j) q -> p j q", j=PACK)

        nc.gpsimd.memset(k_scales[:].bitcast(I32), 0)
        make_identity(nc, ident[:])
        nc.sync.dma_start(q_raw[0][:], query_v[:, :, 0:P])
        for quad in range(QUADRANTS):
            nc.sync.dma_start(
                k_scales[32 * quad : 32 * quad + 4, :].bitcast(I32),
                keys_scales[0, 4 * quad : 4 * quad + 4, :].bitcast(I32),
            )
        nc.sync.dma_start(k_words[0][:].bitcast(I32), keys_words[0, :, 0:T].bitcast(I32))
        nc.sync.dma_start(q_raw[1][:], query_v[:, :, P : 2 * P])
        nc.sync.dma_start(k_words[1][:].bitcast(I32), keys_words[0, :, T : 2 * T].bitcast(I32))
        nc.sync.dma_start(list4[:], offs4)
        nc.vector.memset(mgain_sb[:], 0.0)
        nc.sync.dma_start(mgain_sb[0:1, :], mgain[0:1, :])
        nc.sync.dma_start(lists[0][:], offs)
        nc.sync.dma_start(lists[1][:], offs2)
        nc.sync.dma_start(lists[2][:], offs3)
        nc.sync.dma_start(vals_sb[0][:], vals_v[:, 0, :])
        nc.sync.dma_start(lam_sb[0][:], lam[0:P, :])
        nc.sync.dma_start(vals_sb[1][:], vals_v[:, 1, :])
        nc.sync.dma_start(os_sb[:], slot_factor.rearrange("o (p t) -> p (o t)", t=PACK))
        nc.sync.dma_start(lam_sb[1][:], lam[P : 2 * P, :])
        for j in range(2, PACK):
            nc.sync.dma_start(vals_sb[j][:], vals_v[:, j, :])
        for j in range(PACK):
            nc.sync.dma_start(member_sb[j][:], member_v[:, j, :])

        gain_row = sb([P, Q], F32, "gain_row")
        gather_on_scalar(gain_row[:], mgain_sb, list4[:])

        q_bf = [sb([P, P, PACK], BF16, f"q_bf{b}") for b in range(QB)]
        q_codes = [sb([P, P], U32, f"q_codes{b}") for b in range(QB)]
        q_scales = [sb([P, P], U8, f"q_scales{b}") for b in range(QB)]
        for b in range(QB):
            interleave(nc.vector.tensor_copy, q_bf[b][:], q_raw[b][:])
            quantize(q_codes[b], q_scales[b], q_bf[b])

        a_sb = [sb([P, T], F32, f"a{b}", tag=f"a{b}") for b in range(QB)]

        def scores(b, first, width, bank, copy):
            acc = bank[:, 0:width]
            half, byte = divmod(2 * first, T)
            nc.tensor.matmul_mx(
                out=acc,
                lhsT=q_codes[b][:].bitcast(FP8X4),
                lhsT_scale=q_scales[b][:],
                rhs=k_words[half][:, byte : byte + 2 * width].bitcast(FP4X4),
                rhs_scale=k_scales[:, first : first + width],
                start=True,
                stop=True,
            )
            copy(a_sb[b][:, first : first + width], acc)

        widths = (BANK, BANK, BANK, BANK // 2, BANK // 2)
        for n, width in enumerate(widths):
            copy = nc.scalar.copy if n % 2 else nc.vector.tensor_copy
            scores(0, sum(widths[:n]), width, banks[n], copy)
        for c in range(T // BANK):
            scores(1, c * BANK, BANK, banks[(len(widths) + c) % len(banks)], nc.vector.tensor_copy)

        picked = [[sb([P, I], F32, f"picked{b}_{n}") for n in range(3)] for b in range(QB)]
        ring = [sb([P, I], F32, f"ring{n}", tag=f"ring{n}") for n in range(RING)]
        w_dealt = [sb([P, PACK, P], F32, f"w_dealt{b}") for b in range(QB)]
        w_bf = sb([P, Q, PACK], BF16, "w_bf")
        w_scales = sb([P, Q], U8, "w_scales")
        v_codes = [sb([P, 2 * P], U32, f"v_codes{h}") for h in range(2)]
        v_scales = [sb([P, 2 * P], U8, f"v_scales{h}") for h in range(2)]
        gain = sb([P, Q], F32, "gain")
        m_pick = [sb([P, 2, Q], F32, "m_pick0")]
        y = sb([P, PACK, Q], F32, "y")
        y_codes = sb([P, Q], U32, "y_codes")
        y_scales = sb([P, Q], U8, "y_scales")

        def ring_tiles(b):
            return [ring[(n - b) % RING] for n in range(RING)]

        def low_high(b):
            lo, hi = ring_tiles(b)[:2]
            nc.vector.tensor_tensor(hi[:], picked[b][0][:], picked[b][1][:], ALU.max)
            nc.vector.tensor_tensor(lo[:], picked[b][0][:], picked[b][1][:], ALU.min)

        def weights(b):
            lo, hi, mid, med = ring_tiles(b)
            halves = (slice(0, I // 2), slice(I // 2, I))
            for c in halves:
                nc.vector.tensor_tensor(mid[:, c], hi[:, c], picked[b][2][:, c], ALU.min)
            for c in halves:
                nc.vector.tensor_tensor(med[:, c], lo[:, c], mid[:, c], ALU.max)
            for n, c in enumerate(halves):
                nc.vector.tensor_scalar(
                    w_dealt[b][:, :, n * P // 2 : (n + 1) * P // 2].rearrange("p t s -> p s t"),
                    med[:, c].rearrange("p (s t) -> p s t", t=PACK),
                    lam_sb[b][:],
                    0.0,
                    ALU.mult,
                    ALU.max,
                )

        def turn_weights(b):
            turned = banks[b][:].rearrange("s (t q) -> s t q", t=PACK)
            for t in range(PACK):
                nc.tensor.transpose(turned[:, t, :], w_dealt[b][:, t, :], ident[:])
            nc.vector.tensor_tensor(
                w_bf[:, b * P : (b + 1) * P, :],
                turned.rearrange("s t q -> s q t"),
                os_sb[:].unsqueeze(1).to_broadcast([P, P, PACK]),
                ALU.mult,
            )

        def turn_values(bank, picked_pair, turned_pair, copy):
            turned = bank[:].rearrange("s (g u e) -> s g u e", g=2, u=2)
            for g in range(2):
                words = picked_pair[:, g, :].bitcast(F32)
                for u in range(2):
                    nc.tensor.transpose(turned[:, g, u, :], words[:, u : I // 2 : 2], ident[:])
            copy(
                turned_pair[:].rearrange("s c t -> s (c t)").bitcast(F32).rearrange("s (g e u) -> s g e u", g=2, u=2),
                turned.rearrange("s g u e -> s g e u"),
            )

        for n in range(3):
            gather_on_scalar(picked[0][n][:], a_sb[0], lists[n][:])
        for n in range(2):
            gather_on_scalar(picked[1][n][:], a_sb[1], lists[n][:])

        gain_col = sb([P, QB], F32, "gain_col")
        down = banks[3][:, 0:Q].rearrange("q (b r) -> q b r", b=QB)
        for b in range(QB):
            nc.tensor.transpose(down[:, b, :], gain_row[:, b * P : (b + 1) * P], ident[:])
        nc.vector.tensor_copy(gain_col[:], down[:, :, 0])
        for b in range(QB):
            nc.tensor.transpose(
                banks[4][:, b * P : (b + 1) * P], gain_col[:, b : b + 1].to_broadcast([P, P]), ident[:]
            )
        nc.vector.tensor_copy(gain[:], banks[4][:, 0:Q])

        gather_on_vector(picked[1][2][:], a_sb[1], lists[2][:])
        low_high(0)
        weights(0)
        low_high(1)
        turn_weights(0)
        weights(1)

        v_pick = [sb([P, 2, I], BF16, "v_pick0", tag="a1"), sb([P, 2, I], BF16, "v_pick1", tag="last_pick")]
        for j in range(PACK):
            gather_on_scalar(v_pick[j // 2][:, j % 2, :], vals_sb[j], lists[0][:])
        v_bf = [sb([P, 2 * P, PACK], BF16, "v_bf0", tag="ring2")]
        turn_values(banks[0], v_pick[0], v_bf[0], nc.vector.tensor_copy)
        turn_weights(1)
        quantize(v_codes[0], v_scales[0], v_bf[0])
        w_codes = sb([P, Q], U32, "w_codes", tag="vals3")
        quantize(w_codes, w_scales, w_bf)
        gather_on_scalar(m_pick[0][:, 0, :], member_sb[0], list4[:])
        v_bf.append(sb([P, 2 * P, PACK], BF16, "v_bf1", tag="member0"))
        turn_values(banks[2], v_pick[1], v_bf[1], nc.scalar.copy)
        m_pick.append(sb([P, 2, Q], F32, "m_pick1", tag="last_pick"))
        for j in range(1, PACK):
            gather_on_scalar(m_pick[j // 2][:, j % 2, :], member_sb[j], list4[:])
        y_bf = sb([P, Q, PACK], BF16, "y_bf")
        quantize(v_codes[1], v_scales[1], v_bf[1])

        scaled = [sb([P, 2, Q], F32, "scaled0", tag="member0"), sb([P, 2, Q], F32, "scaled1")]
        for h in range(2):
            o_acc = banks[4 + h][:].rearrange("p (g q) -> p g q", g=2)
            for g in range(2):
                nc.tensor.matmul_mx(
                    out=o_acc[:, g, :],
                    lhsT=v_codes[h][:, g * P : (g + 1) * P].bitcast(FP8X4),
                    lhsT_scale=v_scales[h][:, g * P : (g + 1) * P],
                    rhs=w_codes[:].bitcast(FP8X4),
                    rhs_scale=w_scales[:],
                    start=True,
                    stop=True,
                )
            nc.vector.tensor_tensor(scaled[h][:], o_acc, gain[:].unsqueeze(1).to_broadcast([P, 2, Q]), ALU.mult)
        for h in range(2):
            nc.vector.tensor_tensor(y[:, 2 * h : 2 * h + 2, :], scaled[h][:], m_pick[h][:], ALU.add)
            nc.sync.dma_start(out_v[:, 2 * h : 2 * h + 2, :], y[:, 2 * h : 2 * h + 2, :])

        for copy, c in (
            (nc.vector.tensor_copy, slice(0, Y_VECTOR_COLUMNS)),
            (nc.scalar.copy, slice(Y_VECTOR_COLUMNS, Q)),
        ):
            interleave(copy, y_bf[:, c, :], y[:, :, c])
        quantize(y_codes, y_scales, y_bf)
        nc.sync.dma_start(out_1[0].rearrange("p c r -> p (c r)").bitcast(I32), y_codes[:].bitcast(I32))
        for quad in range(QUADRANTS):
            nc.scalar.dma_start(
                out_2[0, 4 * quad : 4 * quad + 4, :].bitcast(I32),
                y_scales[32 * quad : 32 * quad + 4, :].bitcast(I32),
            )
